import numpy as np
import ml_dtypes


def mxq(x, axis, fmt="e4m3"):
    dtype, down = {"e4m3": (ml_dtypes.float8_e4m3fn, 7), "e5m2": (ml_dtypes.float8_e5m2, 14)}[fmt]
    v = np.moveaxis(np.asarray(x, np.float32).astype(ml_dtypes.bfloat16).astype(np.float64), axis, -1)
    blocks = v.reshape(v.shape[:-1] + (-1, 32))
    amax = np.abs(blocks).max(-1, keepdims=True)
    byte = np.maximum(np.where(amax > 0, np.frexp(amax)[1] - 1 + 127, 0) - down, 1)
    scale = np.exp2(byte - 127.0)
    codes = (blocks / scale).astype(np.float32).astype(dtype).astype(np.float64)
    return np.moveaxis((codes * scale).reshape(v.shape), -1, axis)


WIDE = False


def mx_kscale(k, group=512):
    if not WIDE:
        return np.ones(k)
    levels = np.array([18, -18])
    if group != 512:
        return np.exp2(np.random.permutation(np.resize(levels, k // group))).repeat(group)
    if k % 512:
        return np.exp2(np.random.permutation(np.resize(levels, k // 32))).repeat(32)
    a = np.empty((k // 512, 16))
    for p in range(k // 512):
        a[p, :8] = np.random.permutation(np.resize(levels, 8))
        for g in range(8):
            far = levels[np.abs(levels - a[p, g]) >= 10]
            a[p, g + 8] = far[np.random.randint(len(far))]
    return np.exp2(a.ravel()).repeat(32)


def f64(x):
    return np.asarray(x).astype(np.float64)


G, D, M, O, N = 4, 128, 128, 128, 512


def setup_inputs():
    n = np.random.standard_normal
    s_d = mx_kscale(D, 0)
    s_o = mx_kscale(O, 0)
    return {
        "x": (n((G, D, N)) * s_d[:, None]).astype(np.float32),
        "w1": (n((G, D, M)) / np.sqrt(D) / s_d[:, None]).astype(np.float32),
        "w2": (n((G, D, M)) / np.sqrt(D) / s_d[:, None]).astype(np.float32),
        "sh": (np.random.uniform(0.1, 0.4, (G, M, 1))).astype(np.float32),
        "d0": (np.random.uniform(2.0, 6.0, (G, M, N))).astype(np.float32),
        "wo": (n((G, O, M)) / np.sqrt(O) / s_o[:, None]).astype(np.float32),
        "dy": (n((G, O, N)) * s_o[:, None]).astype(np.float32),
        "dx": (n((G, D, N)) * s_d[:, None]).astype(np.float32),
        "og": (np.random.uniform(0.5, 2.0, (G, M, 1))).astype(np.float32),
        "base": (0.3 * n((G, M, N))).astype(np.float32),
    }


def reference(x, w1, w2, sh, d0, wo, dy, dx, og, base):
    w1q = mxq(f64(w1), 1, "e4m3")
    xq = mxq(f64(x), 1, "e4m3")
    z1 = w1q.transpose(0, 2, 1) @ xq
    dxq = mxq(f64(dx), 1, "e4m3")
    tz1 = w1q.transpose(0, 2, 1) @ dxq
    w2q = mxq(f64(w2), 1, "e4m3")
    z2 = w2q.transpose(0, 2, 1) @ xq
    tz2 = w2q.transpose(0, 2, 1) @ dxq
    q1 = f64(d0) - z1 * 2.0
    woq = mxq(f64(wo), 1, "e4m3")
    dyq = mxq(f64(dy), 1, "e4m3")
    c0 = woq.transpose(0, 2, 1) @ dyq
    xq1 = tz1 * 2.0 * (-1.0)
    xdq1 = (tz2 * c0 * np.exp(q1 * f64(sh) * (-1.0)) + xq1 * f64(sh) * (-1.0) * np.exp(q1 * f64(sh) * (-1.0)) * c0 * z2) * (-1.0) * f64(sh)
    xdz1 = xdq1 * (-1.0) * 2.0
    y = xdz1 * f64(og) + f64(base)
    return y

@@ -1,0 +1,194 @@
+from contextlib import ExitStack
+
+import concourse.mybir as mybir
+
+G, D, M, N = 4, 128, 128, 512
+FLOPS = 5 * 2 * G * D * M * N
+
+F32 = mybir.dt.float32
+BF16 = mybir.dt.bfloat16
+U32 = mybir.dt.uint32
+U8 = mybir.dt.uint8
+FP8X4 = mybir.dt.float8_e4m3fn_x4
+ALU = mybir.AluOpType
+ACT = mybir.ActivationFunctionType
+
+P = 128
+PACK = 4
+ROWS = 32
+VECTOR_COLS = 336
+SCALAR_DY_COLS = 384
+
+
+def tile_rows_hvkernrbf_kernel(tc, x, w1, w2, sh, d0, wo, dy, dx, og, base, out):
+    nc = tc.nc
+    with ExitStack() as ctx:
+        sb = ctx.enter_context(tc.tile_pool(name="sb", bufs=1))
+        ps = ctx.enter_context(tc.psum_pool(name="ps", bufs=1))
+        ctx.enter_context(tc.manual_schedule())
+
+        def load_operand(name, src):
+            width = src.shape[2]
+            raw = sb.tile([P, PACK, width], F32, name=name + "_raw", align_bytes=64)
+            nc.sync.dma_start(out=raw[:], in_=src.rearrange("g (p j) c -> (g p) j c", j=PACK))
+            return raw
+
+        def load_group(name, src, g):
+            t = sb.tile([P, N], F32, name="%s_%d" % (name, g), align_bytes=64)
+            nc.sync.dma_start(out=t[:], in_=src[g])
+            return t
+
+        def views(grouped, at, raw, c0, c1):
+            dst = grouped[:, at + c0 : at + c1, :].rearrange("p (c i) j -> p c j i", i=4)
+            src = raw[:, :, c0:c1].rearrange("p j (c i) -> p c j i", i=4)
+            return dst, src
+
+        def cast_vector(*a):
+            dst, src = views(*a)
+            nc.vector.tensor_copy(out=dst, in_=src)
+
+        def cast_scalar(*a):
+            dst, src = views(*a)
+            nc.scalar.copy(out=dst, in_=src)
+
+        def cast_gpsimd(*a):
+            dst, src = views(*a)
+            nc.gpsimd.tensor_scalar(out=dst, in0=src, scalar1=1.0, scalar2=0.0, op0=ALU.mult, op1=ALU.add)
+
+        def operand_tiles(name, width):
+            grouped = sb.tile([P, width, PACK], BF16, name=name + "_bf16", align_bytes=64)
+            codes = sb.tile([P, width], U32, name=name + "_codes", align_bytes=64)
+            scales = sb.tile([P, width], U8, name=name + "_scales", align_bytes=64)
+            return grouped, codes, scales
+
+        def quantize(op):
+            grouped, codes, scales = op
+            nc.vector.quantize_mx(out=codes[:].bitcast(FP8X4), scales=scales[:], in_=grouped[:].rearrange("p c j -> p (c j)"))
+
+        def product(bank, g, wop, at, xop):
+            rows = slice(ROWS * g, ROWS * (g + 1))
+            nc.tensor.matmul_mx(
+                out=bank[:],
+                lhsT=wop[1][rows, at : at + M].bitcast(FP8X4),
+                lhsT_scale=wop[2][rows, at : at + M],
+                rhs=xop[1][rows, :].bitcast(FP8X4),
+                rhs_scale=xop[2][rows, :],
+                start=True,
+                stop=True,
+            )
+
+        def work(name):
+            return [sb.tile([P, N], F32, name="%s_%d" % (name, g), align_bytes=64) for g in range(G)]
+
+        bank_p = [ps.tile([P, N], F32, name="bank_p%d" % g) for g in range(G)]
+        bank_q = [ps.tile([P, N], F32, name="bank_q%d" % g) for g in range(G)]
+        xq, dxq, dyq = operand_tiles("x", N), operand_tiles("dx", N), operand_tiles("dy", N)
+        w21q, woq = operand_tiles("w21", 2 * M), operand_tiles("wo", M)
+        a, q, e, b, c, ge, r, o = [work(n) for n in ("a", "q", "e", "b", "c", "ge", "r", "o")]
+
+        vec_rows = sb.tile([P, P], F32, align_bytes=64)
+        vec_cols = sb.tile([P, P], F32, align_bytes=64)
+        gain = sb.tile([P, G], F32, align_bytes=64)
+        nc.vector.memset(vec_rows[:], 0.0)
+        x_raw = load_operand("x", x)
+        for row, src in enumerate((sh, og)):
+            nc.sync.dma_start(
+                out=vec_rows[row:P:ROWS, :].rearrange("b (g r) -> b g r", g=G),
+                in_=src.rearrange("g (b r) o -> b g (r o)", r=ROWS),
+            )
+        w2_raw = load_operand("w2", w2)
+        w1_raw = load_operand("w1", w1)
+        dx_raw = load_operand("dx", dx)
+        d0_sb = [load_group("d0", d0, g) for g in range(2)]
+        wo_raw = load_operand("wo", wo)
+        dy_raw = load_operand("dy", dy)
+        d0_sb = d0_sb + [load_group("d0", d0, g) for g in range(2, G)]
+        base_sb = [load_group("base", base, g) for g in range(G)]
+
+        by_group = vec_cols[:].rearrange("p (g r) -> p g r", g=G)
+        sh_col = [vec_cols[:, ROWS * g : ROWS * g + 1] for g in range(G)]
+
+        cast_vector(xq[0], 0, x_raw, 0, VECTOR_COLS)
+        cast_scalar(xq[0], 0, x_raw, VECTOR_COLS, N)
+        nc.vector.transpose(out=vec_cols[:], in_=vec_rows[:])
+        quantize(xq)
+        cast_scalar(w21q[0], 0, w2_raw, 0, M)
+        cast_vector(w21q[0], M, w1_raw, 0, M)
+        nc.vector.scalar_tensor_tensor(out=gain[:], in0=by_group[:, :, 0], scalar=2.0, in1=by_group[:, :, 1], op0=ALU.mult, op1=ALU.mult)
+        quantize(w21q)
+        for g in range(G):
+            product(bank_p[g], g, w21q, 0, xq)
+            product(bank_q[g], g, w21q, M, xq)
+
+        def step_a(g):
+            nc.scalar.activation(out=a[g][:], in_=bank_p[g][:], func=ACT.Copy, scale=sh_col[g])
+
+        def step_q(g):
+            nc.vector.scalar_tensor_tensor(out=q[g][:], in0=bank_q[g][:], scalar=2.0, in1=d0_sb[g][:], op0=ALU.mult, op1=ALU.subtract)
+            product(bank_q[g], g, w21q, 0, dxq)
+
+        def step_exp(g):
+            nc.scalar.activation(out=e[g][:], in_=q[g][:], func=ACT.Exp, scale=sh_col[g])
+
+        def step_b(g):
+            nc.vector.scalar_tensor_tensor(out=b[g][:], in0=bank_p[g][:], scalar=2.0, in1=a[g][:], op0=ALU.mult, op1=ALU.mult)
+
+        def step_c(g):
+            nc.vector.tensor_tensor(out=c[g][:], in0=bank_q[g][:], in1=b[g][:], op=ALU.add)
+
+        def step_ge(g):
+            nc.gpsimd.tensor_tensor(out=ge[g][:], in0=c[g][:], in1=e[g][:], op=ALU.mult)
+
+        def step_r(g):
+            nc.vector.scalar_tensor_tensor(out=r[g][:], in0=bank_p[g][:], scalar=gain[:, g : g + 1], in1=ge[g][:], op0=ALU.mult, op1=ALU.mult)
+
+        def step_out(g, engine):
+            engine.tensor_tensor(out=o[g][:], in0=r[g][:], in1=base_sb[g][:], op=ALU.add)
+            nc.sync.dma_start(out=out[g], in_=o[g][:])
+
+        step_a(0)
+        cast_vector(dxq[0], 0, dx_raw, 0, VECTOR_COLS)
+        cast_scalar(dxq[0], 0, dx_raw, VECTOR_COLS, N)
+        step_a(1)
+        quantize(dxq)
+        for g in range(2):
+            product(bank_p[g], g, w21q, M, dxq)
+        step_q(0)
+        step_exp(0)
+        cast_gpsimd(woq[0], 0, wo_raw, 0, M)
+        step_b(0)
+        step_c(0)
+        step_ge(0)
+        for g in range(2, G):
+            step_a(g)
+            product(bank_p[g], g, w21q, M, dxq)
+        step_q(1)
+        step_exp(1)
+        step_b(1)
+        step_c(1)
+        cast_scalar(dyq[0], 0, dy_raw, 0, SCALAR_DY_COLS)
+        cast_gpsimd(dyq[0], 0, dy_raw, SCALAR_DY_COLS, N)
+        step_ge(1)
+        step_q(2)
+        step_exp(2)
+        step_b(2)
+        quantize(woq)
+        quantize(dyq)
+        for g in range(3):
+            product(bank_p[g], g, woq, 0, dyq)
+        step_c(2)
+        step_ge(2)
+        step_r(0)
+        step_out(0, nc.gpsimd)
+        step_q(3)
+        step_exp(3)
+        step_b(3)
+        product(bank_p[3], 3, woq, 0, dyq)
+        step_c(3)
+        step_ge(3)
+        step_r(1)
+        step_out(1, nc.gpsimd)
+        step_r(2)
+        step_r(3)
+        step_out(2, nc.vector)
+        step_out(3, nc.vector)

@@ -39,8 +39,8 @@ def tile_rows_hvkernrbf_kernel(tc, x, w1, w2, sh, d0, wo, dy, dx, og, base, out)
             return t
 
         def views(grouped, at, raw, c0, c1):
-            dst = grouped[:, at + c0 : at + c1, :].rearrange("p (c i) j -> p c j i", i=4)
-            src = raw[:, :, c0:c1].rearrange("p j (c i) -> p c j i", i=4)
+            dst = grouped[:, at + c0 : at + c1, :].rearrange("p (c i) j -> p c j i", i=2)
+            src = raw[:, :, c0:c1].rearrange("p j (c i) -> p c j i", i=2)
             return dst, src
 
         def cast_vector(*a):
@@ -83,7 +83,7 @@ def tile_rows_hvkernrbf_kernel(tc, x, w1, w2, sh, d0, wo, dy, dx, og, base, out)
         bank_p = [ps.tile([P, N], F32, name="bank_p%d" % g) for g in range(G)]
         bank_q = [ps.tile([P, N], F32, name="bank_q%d" % g) for g in range(G)]
         xq, dxq, dyq = operand_tiles("x", N), operand_tiles("dx", N), operand_tiles("dy", N)
-        w21q, woq = operand_tiles("w21", 2 * M), operand_tiles("wo", M)
+        w1q, w2q, woq = operand_tiles("w1", M), operand_tiles("w2", M), operand_tiles("wo", M)
         a, q, e, b, c, ge, r, o = [work(n) for n in ("a", "q", "e", "b", "c", "ge", "r", "o")]
 
         vec_rows = sb.tile([P, P], F32, align_bytes=64)
@@ -99,33 +99,21 @@ def tile_rows_hvkernrbf_kernel(tc, x, w1, w2, sh, d0, wo, dy, dx, og, base, out)
         w2_raw = load_operand("w2", w2)
         w1_raw = load_operand("w1", w1)
         dx_raw = load_operand("dx", dx)
-        d0_sb = [load_group("d0", d0, g) for g in range(2)]
+        d0_sb = [load_group("d0", d0, 0)]
         wo_raw = load_operand("wo", wo)
+        d0_sb = d0_sb + [load_group("d0", d0, g) for g in (1, 2)]
         dy_raw = load_operand("dy", dy)
-        d0_sb = d0_sb + [load_group("d0", d0, g) for g in range(2, G)]
+        d0_sb = d0_sb + [load_group("d0", d0, 3)]
         base_sb = [load_group("base", base, g) for g in range(G)]
 
         by_group = vec_cols[:].rearrange("p (g r) -> p g r", g=G)
         sh_col = [vec_cols[:, ROWS * g : ROWS * g + 1] for g in range(G)]
-
-        cast_vector(xq[0], 0, x_raw, 0, VECTOR_COLS)
-        cast_scalar(xq[0], 0, x_raw, VECTOR_COLS, N)
-        nc.vector.transpose(out=vec_cols[:], in_=vec_rows[:])
-        quantize(xq)
-        cast_scalar(w21q[0], 0, w2_raw, 0, M)
-        cast_vector(w21q[0], M, w1_raw, 0, M)
-        nc.vector.scalar_tensor_tensor(out=gain[:], in0=by_group[:, :, 0], scalar=2.0, in1=by_group[:, :, 1], op0=ALU.mult, op1=ALU.mult)
-        quantize(w21q)
-        for g in range(G):
-            product(bank_p[g], g, w21q, 0, xq)
-            product(bank_q[g], g, w21q, M, xq)
 
         def step_a(g):
             nc.scalar.activation(out=a[g][:], in_=bank_p[g][:], func=ACT.Copy, scale=sh_col[g])
 
         def step_q(g):
             nc.vector.scalar_tensor_tensor(out=q[g][:], in0=bank_q[g][:], scalar=2.0, in1=d0_sb[g][:], op0=ALU.mult, op1=ALU.subtract)
-            product(bank_q[g], g, w21q, 0, dxq)
 
         def step_exp(g):
             nc.scalar.activation(out=e[g][:], in_=q[g][:], func=ACT.Exp, scale=sh_col[g])
@@ -146,49 +134,80 @@ def tile_rows_hvkernrbf_kernel(tc, x, w1, w2, sh, d0, wo, dy, dx, og, base, out)
             engine.tensor_tensor(out=o[g][:], in0=r[g][:], in1=base_sb[g][:], op=ALU.add)
             nc.sync.dma_start(out=out[g], in_=o[g][:])
 
+        def step_out_cols(g, engine, c0, c1, store):
+            engine.tensor_tensor(out=o[g][:, c0:c1], in0=r[g][:, c0:c1], in1=base_sb[g][:, c0:c1], op=ALU.add)
+            if store:
+                nc.sync.dma_start(out=out[g][:, store[0] : store[1]], in_=o[g][:, store[0] : store[1]])
+
+        def step_q_off(g):
+            nc.scalar.activation(out=u[g][:], in_=bank_q[g][:], func=ACT.Copy, scale=2.0)
+            nc.gpsimd.tensor_tensor(out=q[g][:], in0=u[g][:], in1=d0_sb[g][:], op=ALU.subtract)
+
+        u = work("u")
+        cast_vector(xq[0], 0, x_raw, 0, VECTOR_COLS)
+        cast_scalar(xq[0], 0, x_raw, VECTOR_COLS, N)
+        nc.vector.transpose(out=vec_cols[:], in_=vec_rows[:])
+        quantize(xq)
+        cast_scalar(w2q[0], 0, w2_raw, 0, M)
+        quantize(w2q)
+        for g in range(2):
+            product(bank_p[g], g, w2q, 0, xq)
+        cast_scalar(w1q[0], 0, w1_raw, 0, M)
+        nc.vector.scalar_tensor_tensor(out=gain[:], in0=by_group[:, :, 0], scalar=2.0, in1=by_group[:, :, 1], op0=ALU.mult, op1=ALU.mult)
+        quantize(w1q)
+        for g in range(3):
+            product(bank_q[g], g, w1q, 0, xq)
+        product(bank_p[2], 2, w2q, 0, xq)
+        product(bank_p[3], 3, w2q, 0, xq)
         step_a(0)
         cast_vector(dxq[0], 0, dx_raw, 0, VECTOR_COLS)
         cast_scalar(dxq[0], 0, dx_raw, VECTOR_COLS, N)
         step_a(1)
-        quantize(dxq)
-        for g in range(2):
-            product(bank_p[g], g, w21q, M, dxq)
         step_q(0)
+        quantize(dxq)
+        product(bank_p[0], 0, w1q, 0, dxq)
+        product(bank_p[1], 1, w1q, 0, dxq)
+        product(bank_q[0], 0, w2q, 0, dxq)
+        step_q(1)
+        product(bank_q[1], 1, w2q, 0, dxq)
+        cast_scalar(woq[0], 0, wo_raw, 0, M)
+        quantize(woq)
+        product(bank_q[3], 3, w1q, 0, xq)
+        step_q_off(2)
+        product(bank_q[2], 2, w2q, 0, dxq)
+        step_a(2)
+        product(bank_p[2], 2, w1q, 0, dxq)
         step_exp(0)
-        cast_gpsimd(woq[0], 0, wo_raw, 0, M)
+        step_a(3)
+        product(bank_p[3], 3, w1q, 0, dxq)
+        step_exp(1)
         step_b(0)
+        step_b(1)
         step_c(0)
         step_ge(0)
-        for g in range(2, G):
-            step_a(g)
-            product(bank_p[g], g, w21q, M, dxq)
-        step_q(1)
-        step_exp(1)
-        step_b(1)
         step_c(1)
-        cast_scalar(dyq[0], 0, dy_raw, 0, SCALAR_DY_COLS)
-        cast_gpsimd(dyq[0], 0, dy_raw, SCALAR_DY_COLS, N)
         step_ge(1)
-        step_q(2)
-        step_exp(2)
+        cast_scalar(dyq[0], 0, dy_raw, 0, N)
         step_b(2)
-        quantize(woq)
-        quantize(dyq)
-        for g in range(3):
-            product(bank_p[g], g, woq, 0, dyq)
-        step_c(2)
-        step_ge(2)
-        step_r(0)
-        step_out(0, nc.gpsimd)
         step_q(3)
+        product(bank_q[3], 3, w2q, 0, dxq)
+        step_exp(2)
         step_exp(3)
         step_b(3)
-        product(bank_p[3], 3, woq, 0, dyq)
+        step_c(2)
+        quantize(dyq)
+        for g in range(4):
+            product(bank_p[g], g, woq, 0, dyq)
+        step_ge(2)
         step_c(3)
         step_ge(3)
+        step_r(0)
         step_r(1)
-        step_out(1, nc.gpsimd)
+        step_out_cols(0, nc.gpsimd, 0, 256, None)
         step_r(2)
         step_r(3)
+        step_out_cols(0, nc.vector, 256, 512, (0, 512))
+        step_out(1, nc.vector)
         step_out(2, nc.vector)
-        step_out(3, nc.vector)
+        step_out_cols(3, nc.vector, 0, 256, (0, 256))
+        step_out_cols(3, nc.vector, 256, 512, (256, 512))

from contextlib import ExitStack

import concourse.mybir as mybir

G, D, M, N = 4, 128, 128, 512
FLOPS = 5 * 2 * G * D * M * N

F32 = mybir.dt.float32
BF16 = mybir.dt.bfloat16
U32 = mybir.dt.uint32
U8 = mybir.dt.uint8
FP8X4 = mybir.dt.float8_e4m3fn_x4
ALU = mybir.AluOpType
ACT = mybir.ActivationFunctionType

P = 128
PACK = 4
ROWS = 32
VECTOR_COLS = 336
SCALAR_DY_COLS = 384


def tile_rows_hvkernrbf_kernel(tc, x, w1, w2, sh, d0, wo, dy, dx, og, base, out):
    nc = tc.nc
    with ExitStack() as ctx:
        sb = ctx.enter_context(tc.tile_pool(name="sb", bufs=1))
        ps = ctx.enter_context(tc.psum_pool(name="ps", bufs=1))
        ctx.enter_context(tc.manual_schedule())

        def load_operand(name, src):
            width = src.shape[2]
            raw = sb.tile([P, PACK, width], F32, name=name + "_raw", align_bytes=64)
            nc.sync.dma_start(out=raw[:], in_=src.rearrange("g (p j) c -> (g p) j c", j=PACK))
            return raw

        def load_group(name, src, g):
            t = sb.tile([P, N], F32, name="%s_%d" % (name, g), align_bytes=64)
            nc.sync.dma_start(out=t[:], in_=src[g])
            return t

        def views(grouped, at, raw, c0, c1):
            dst = grouped[:, at + c0 : at + c1, :].rearrange("p (c i) j -> p c j i", i=2)
            src = raw[:, :, c0:c1].rearrange("p j (c i) -> p c j i", i=2)
            return dst, src

        def cast_vector(*a):
            dst, src = views(*a)
            nc.vector.tensor_copy(out=dst, in_=src)

        def cast_scalar(*a):
            dst, src = views(*a)
            nc.scalar.copy(out=dst, in_=src)

        def cast_gpsimd(*a):
            dst, src = views(*a)
            nc.gpsimd.tensor_scalar(out=dst, in0=src, scalar1=1.0, scalar2=0.0, op0=ALU.mult, op1=ALU.add)

        def operand_tiles(name, width):
            grouped = sb.tile([P, width, PACK], BF16, name=name + "_bf16", align_bytes=64)
            codes = sb.tile([P, width], U32, name=name + "_codes", align_bytes=64)
            scales = sb.tile([P, width], U8, name=name + "_scales", align_bytes=64)
            return grouped, codes, scales

        def quantize(op):
            grouped, codes, scales = op
            nc.vector.quantize_mx(out=codes[:].bitcast(FP8X4), scales=scales[:], in_=grouped[:].rearrange("p c j -> p (c j)"))

        def product(bank, g, wop, at, xop):
            rows = slice(ROWS * g, ROWS * (g + 1))
            nc.tensor.matmul_mx(
                out=bank[:],
                lhsT=wop[1][rows, at : at + M].bitcast(FP8X4),
                lhsT_scale=wop[2][rows, at : at + M],
                rhs=xop[1][rows, :].bitcast(FP8X4),
                rhs_scale=xop[2][rows, :],
                start=True,
                stop=True,
            )

        def work(name):
            return [sb.tile([P, N], F32, name="%s_%d" % (name, g), align_bytes=64) for g in range(G)]

        bank_p = [ps.tile([P, N], F32, name="bank_p%d" % g) for g in range(G)]
        bank_q = [ps.tile([P, N], F32, name="bank_q%d" % g) for g in range(G)]
        xq, dxq, dyq = operand_tiles("x", N), operand_tiles("dx", N), operand_tiles("dy", N)
        w1q, w2q, woq = operand_tiles("w1", M), operand_tiles("w2", M), operand_tiles("wo", M)
        a, q, e, b, c, ge, r, o = [work(n) for n in ("a", "q", "e", "b", "c", "ge", "r", "o")]

        vec_rows = sb.tile([P, P], F32, align_bytes=64)
        vec_cols = sb.tile([P, P], F32, align_bytes=64)
        gain = sb.tile([P, G], F32, align_bytes=64)
        nc.vector.memset(vec_rows[:], 0.0)
        x_raw = load_operand("x", x)
        for row, src in enumerate((sh, og)):
            nc.sync.dma_start(
                out=vec_rows[row:P:ROWS, :].rearrange("b (g r) -> b g r", g=G),
                in_=src.rearrange("g (b r) o -> b g (r o)", r=ROWS),
            )
        w2_raw = load_operand("w2", w2)
        w1_raw = load_operand("w1", w1)
        dx_raw = load_operand("dx", dx)
        d0_sb = [load_group("d0", d0, 0)]
        wo_raw = load_operand("wo", wo)
        d0_sb = d0_sb + [load_group("d0", d0, g) for g in (1, 2)]
        dy_raw = load_operand("dy", dy)
        d0_sb = d0_sb + [load_group("d0", d0, 3)]
        base_sb = [load_group("base", base, g) for g in range(G)]

        by_group = vec_cols[:].rearrange("p (g r) -> p g r", g=G)
        sh_col = [vec_cols[:, ROWS * g : ROWS * g + 1] for g in range(G)]

        def step_a(g):
            nc.scalar.activation(out=a[g][:], in_=bank_p[g][:], func=ACT.Copy, scale=sh_col[g])

        def step_q(g):
            nc.vector.scalar_tensor_tensor(out=q[g][:], in0=bank_q[g][:], scalar=2.0, in1=d0_sb[g][:], op0=ALU.mult, op1=ALU.subtract)

        def step_exp(g):
            nc.scalar.activation(out=e[g][:], in_=q[g][:], func=ACT.Exp, scale=sh_col[g])

        def step_b(g):
            nc.vector.scalar_tensor_tensor(out=b[g][:], in0=bank_p[g][:], scalar=2.0, in1=a[g][:], op0=ALU.mult, op1=ALU.mult)

        def step_c(g):
            nc.vector.tensor_tensor(out=c[g][:], in0=bank_q[g][:], in1=b[g][:], op=ALU.add)

        def step_ge(g):
            nc.gpsimd.tensor_tensor(out=ge[g][:], in0=c[g][:], in1=e[g][:], op=ALU.mult)

        def step_r(g):
            nc.vector.scalar_tensor_tensor(out=r[g][:], in0=bank_p[g][:], scalar=gain[:, g : g + 1], in1=ge[g][:], op0=ALU.mult, op1=ALU.mult)

        def step_out(g, engine):
            engine.tensor_tensor(out=o[g][:], in0=r[g][:], in1=base_sb[g][:], op=ALU.add)
            nc.sync.dma_start(out=out[g], in_=o[g][:])

        def step_out_cols(g, engine, c0, c1, store):
            engine.tensor_tensor(out=o[g][:, c0:c1], in0=r[g][:, c0:c1], in1=base_sb[g][:, c0:c1], op=ALU.add)
            if store:
                nc.sync.dma_start(out=out[g][:, store[0] : store[1]], in_=o[g][:, store[0] : store[1]])

        def step_q_off(g):
            nc.scalar.activation(out=u[g][:], in_=bank_q[g][:], func=ACT.Copy, scale=2.0)
            nc.gpsimd.tensor_tensor(out=q[g][:], in0=u[g][:], in1=d0_sb[g][:], op=ALU.subtract)

        u = work("u")
        cast_vector(xq[0], 0, x_raw, 0, VECTOR_COLS)
        cast_scalar(xq[0], 0, x_raw, VECTOR_COLS, N)
        nc.vector.transpose(out=vec_cols[:], in_=vec_rows[:])
        quantize(xq)
        cast_scalar(w2q[0], 0, w2_raw, 0, M)
        quantize(w2q)
        for g in range(2):
            product(bank_p[g], g, w2q, 0, xq)
        cast_scalar(w1q[0], 0, w1_raw, 0, M)
        nc.vector.scalar_tensor_tensor(out=gain[:], in0=by_group[:, :, 0], scalar=2.0, in1=by_group[:, :, 1], op0=ALU.mult, op1=ALU.mult)
        quantize(w1q)
        for g in range(3):
            product(bank_q[g], g, w1q, 0, xq)
        product(bank_p[2], 2, w2q, 0, xq)
        product(bank_p[3], 3, w2q, 0, xq)
        step_a(0)
        cast_vector(dxq[0], 0, dx_raw, 0, VECTOR_COLS)
        cast_scalar(dxq[0], 0, dx_raw, VECTOR_COLS, N)
        step_a(1)
        step_q(0)
        quantize(dxq)
        product(bank_p[0], 0, w1q, 0, dxq)
        product(bank_p[1], 1, w1q, 0, dxq)
        product(bank_q[0], 0, w2q, 0, dxq)
        step_q(1)
        product(bank_q[1], 1, w2q, 0, dxq)
        cast_scalar(woq[0], 0, wo_raw, 0, M)
        quantize(woq)
        product(bank_q[3], 3, w1q, 0, xq)
        step_q_off(2)
        product(bank_q[2], 2, w2q, 0, dxq)
        step_a(2)
        product(bank_p[2], 2, w1q, 0, dxq)
        step_exp(0)
        step_a(3)
        product(bank_p[3], 3, w1q, 0, dxq)
        step_exp(1)
        step_b(0)
        step_b(1)
        step_c(0)
        step_ge(0)
        step_c(1)
        step_ge(1)
        cast_scalar(dyq[0], 0, dy_raw, 0, N)
        step_b(2)
        step_q(3)
        product(bank_q[3], 3, w2q, 0, dxq)
        step_exp(2)
        step_exp(3)
        step_b(3)
        step_c(2)
        quantize(dyq)
        for g in range(4):
            product(bank_p[g], g, woq, 0, dyq)
        step_ge(2)
        step_c(3)
        step_ge(3)
        step_r(0)
        step_r(1)
        step_out_cols(0, nc.gpsimd, 0, 256, None)
        step_r(2)
        step_r(3)
        step_out_cols(0, nc.vector, 256, 512, (0, 512))
        step_out(1, nc.vector)
        step_out(2, nc.vector)
        step_out_cols(3, nc.vector, 0, 256, (0, 256))
        step_out_cols(3, nc.vector, 256, 512, (256, 512))
